import numpy as np
import ml_dtypes


def mxq(x, axis, fmt="e4m3"):
    dtype, down = {"e4m3": (ml_dtypes.float8_e4m3fn, 7), "e5m2": (ml_dtypes.float8_e5m2, 14)}[fmt]
    v = np.moveaxis(np.asarray(x, np.float32).astype(ml_dtypes.bfloat16).astype(np.float64), axis, -1)
    blocks = v.reshape(v.shape[:-1] + (-1, 32))
    amax = np.abs(blocks).max(-1, keepdims=True)
    byte = np.maximum(np.where(amax > 0, np.frexp(amax)[1] - 1 + 127, 0) - down, 1)
    scale = np.exp2(byte - 127.0)
    codes = (blocks / scale).astype(np.float32).astype(dtype).astype(np.float64)
    return np.moveaxis((codes * scale).reshape(v.shape), -1, axis)


WIDE = False


def mx_kscale(k):
    if not WIDE:
        return np.ones(k)
    levels = np.array([10, -10, 5, -5, 0])
    if k % 512:
        return np.exp2(np.random.permutation(np.resize(levels, k // 32))).repeat(32)
    a = np.empty((k // 512, 16))
    for p in range(k // 512):
        a[p, :8] = np.random.permutation(np.resize(levels, 8))
        for g in range(8):
            far = levels[np.abs(levels - a[p, g]) >= 10]
            a[p, g + 8] = far[np.random.randint(len(far))]
    return np.exp2(a.ravel()).repeat(32)


def f64(x):
    return np.asarray(x).astype(np.float64)


def striped(idx):
    return np.tile(idx.reshape(-1, 16).T, (8, 1)).astype(np.uint16)


def unstriped(offs):
    return offs[:16].T.reshape(-1).astype(np.int64)


def pack_weight(w):
    k, n = w.shape
    w = f64(np.asarray(w, np.float32).astype(ml_dtypes.bfloat16)).reshape(k // 32, 32, n)
    amax = np.abs(w).max(1)
    byte = np.clip(np.where(amax > 0, np.frexp(amax)[1] - 1 + 127 - 7, 1), 1, 254)
    scaled = (w * np.exp2(127.0 - byte)[:, None, :]).reshape(k, n).astype(np.float32)
    words = np.ascontiguousarray(scaled.reshape(k // 512, 128, 4, n).transpose(0, 1, 3, 2)).astype(ml_dtypes.float8_e4m3fn).view(np.uint8)
    return words, np.ascontiguousarray(byte.astype(np.uint8).reshape(k // 512, 16, n))


def unpack_weight(words, scales):
    g, p, n, _ = words.shape
    vals = np.ascontiguousarray(words).view(ml_dtypes.float8_e4m3fn).astype(np.float64) * np.repeat(np.exp2(scales.astype(np.float64) - 127.0), 8, axis=1)[..., None]
    return vals.transpose(0, 1, 3, 2).reshape(g * 512, n)


K, T, E, C, N = 1024, 512, 4, 128, 256


def by_expert(wq, xq):
    return np.concatenate([wq[e].T @ xq[:, e * C:(e + 1) * C] for e in range(E)], axis=1)


def setup_inputs():
    n = np.random.standard_normal
    s = mx_kscale(K)[:, None]
    packed = [pack_weight(m) for m in n((E, K, N)) / np.sqrt(K) / s[None]]
    return {
        "xT": (n((K, T)) * s).astype(np.float32),
        "w_words": np.stack([m[0] for m in packed]),
        "w_scales": np.stack([m[1] for m in packed]),
        "gate": np.tile(np.random.uniform(0.2, 1.0, E * C), (N, 1)).astype(np.float32),
        "offs": striped(np.random.permutation(T)[:E * C]),
    }


def reference(xT, w_words, w_scales, gate, offs):
    idx = unstriped(offs)
    xq = mxq(f64(xT)[:, idx], 0, "e4m3")
    w = np.stack([unpack_weight(w_words[e], w_scales[e]) for e in range(E)])
    y = by_expert(w, xq)
    out = np.zeros((N, T))
    out[:, idx] = f64(gate) * y
    return out

@@ -1,0 +1,177 @@
+from contextlib import ExitStack
+
+import concourse.mybir as mybir
+
+K, T, E, C, N = 1024, 512, 4, 128, 256
+FLOPS = 2 * K * N * E * C
+
+F32 = mybir.dt.float32
+BF16 = mybir.dt.bfloat16
+U32 = mybir.dt.uint32
+I32 = mybir.dt.int32
+U16 = mybir.dt.uint16
+U8 = mybir.dt.uint8
+FP8X4 = mybir.dt.float8_e4m3fn_x4
+MULT = mybir.AluOpType.mult
+ADD = mybir.AluOpType.add
+
+P = 128
+PASSES = K // 512
+HALF = 256
+
+CAST = {
+    (0, 0): [("v", 0, 320), ("s", 320, 512)],
+    (0, 1): [("s", 0, 288), ("g", 288, 512)],
+    (1, 0): [("s", 0, 288), ("g", 288, 512)],
+    (1, 1): [("s", 0, 288), ("g", 288, 512)],
+}
+LOADS = [
+    ("x", 0, 0, 0, 512),
+    ("o", 0, 0, 0, 0),
+    ("x", 0, 1, 0, 512),
+    ("x", 1, 0, 0, 512),
+    ("x", 1, 1, 0, 512),
+    ("s", 0, 0, 0, 0),
+    ("w", 0, 2, 0, 0),
+    ("g", 0, 0, 0, 0),
+    ("w", 2, 4, 0, 0),
+    ("g", 1, 0, 0, 0),
+]
+
+
+def tile_routed_moe_kernel(tc, xT, w_words, w_scales, gate, offs, out):
+    nc = tc.nc
+    with ExitStack() as ctx:
+        held = ctx.enter_context(tc.tile_pool(name="held", bufs=1))
+        psum = ctx.enter_context(tc.psum_pool(name="psum", bufs=1))
+
+        lists = held.tile([P, T // 16], U16, name="lists")
+
+        x_view = xT.rearrange("(a p u e) t -> a u p e t", a=PASSES, p=P, u=2, e=2)
+        raw = {}
+        for a in range(PASSES):
+            for u in range(2):
+                raw[(a, u)] = held.tile([P, 2, T], F32, name="raw%d%d" % (a, u))
+        w_sc = held.tile([P, E * PASSES, N], U8, name="w_sc", align_bytes=64)
+        nc.vector.memset(w_sc[:].rearrange("p g n -> p (g n)").bitcast(I32), 0)
+        w_cd = held.tile([P, E * PASSES, N], I32, name="w_cd", align_bytes=64)
+        gate_sb = [held.tile([P, T], F32, name="gate%d" % fb) for fb in range(2)]
+
+        for what, i, j, t0, t1 in LOADS:
+            if what == "o":
+                nc.sync.dma_start(lists[:], offs)
+            elif what == "x":
+                nc.sync.dma_start(raw[(i, j)][:, :, t0:t1], x_view[i, j][:, :, t0:t1])
+            elif what == "s":
+                for q in range(4):
+                    nc.sync.dma_start(
+                        w_sc[32 * q : 32 * q + 4].bitcast(I32),
+                        w_scales[:, :, 4 * q : 4 * q + 4, :].rearrange("e a r n -> r (e a) n").bitcast(I32),
+                    )
+            elif what == "w":
+                nc.sync.dma_start(
+                    w_cd[:, i * PASSES : j * PASSES, :],
+                    w_words[i:j].rearrange("e a p n r -> p (e a) (n r)").bitcast(I32),
+                )
+            else:
+                nc.sync.dma_start(gate_sb[i][:], gate[i * P : (i + 1) * P, :])
+
+        pairs = held.tile([P, 5, T, 2], BF16, name="pairs")
+        words = pairs[:].rearrange("p m t e -> p (m t e)").bitcast(U32)
+
+        def slot_of(a, u):
+            return 3 - (2 * a + u)
+
+        for a in range(PASSES):
+            for u in range(2):
+                src = raw[(a, u)][:].rearrange("p e t -> p t e")
+                m = slot_of(a, u)
+                for eng, t0, t1 in CAST[(a, u)]:
+                    if eng == "v":
+                        nc.vector.tensor_copy(out=pairs[:, m, t0:t1, :], in_=src[:, t0:t1, :])
+                    elif eng == "s":
+                        nc.scalar.copy(out=pairs[:, m, t0:t1, :], in_=src[:, t0:t1, :])
+                    else:
+                        nc.gpsimd.tensor_scalar(
+                            out=pairs[:, m, t0:t1, :], in0=src[:, t0:t1, :], scalar1=1.0, scalar2=0.0, op0=MULT, op1=ADD
+                        )
+
+        grouped, x_cd, x_sc = [], [], []
+        for a in range(PASSES):
+            grouped.append(held.tile([P, T, 4], BF16, name="grouped%d" % a, align_bytes=64))
+            x_cd.append(held.tile([P, T], U32, name="x_cd%d" % a, align_bytes=64))
+            x_sc.append(held.tile([P, T], U8, name="x_sc%d" % a, align_bytes=64))
+
+        picked = [held.tile([P, 2, T], U32, name="picked%d" % a) for a in range(PASSES)]
+
+        def gather(a, u, j0, j1):
+            m = slot_of(a, u)
+            width = T if j1 - j0 < T else 2 * T
+            win = words[:, m * T : m * T + width]
+            nc.vector.tensor_copy(out=picked[a][:, u, j0:j1], in_=win.indirect(lists[:, j0 // 16 : j1 // 16]))
+
+        def interleave(a, j0, j1):
+            dst = grouped[a][:].rearrange("p c j -> p (c j)").bitcast(U32).rearrange("p (c u) -> p c u", u=2)
+            nc.scalar.copy(out=dst[:, j0:j1, :], in_=picked[a][:, :, j0:j1].rearrange("p u c -> p c u"))
+
+        def quantize(a, j0, j1):
+            nc.vector.quantize_mx(
+                out=x_cd[a][:, j0:j1].bitcast(FP8X4),
+                scales=x_sc[a][:, j0:j1],
+                in_=grouped[a][:, j0:j1, :].rearrange("p c j -> p (c j)"),
+            )
+
+        acc = {}
+        y_sb = {}
+        window = []
+        for fb in range(2):
+            window.append(held.tile([P, T], F32, name="window%d" % fb))
+            for h in range(2):
+                y_sb[(fb, h)] = held.tile([P, HALF], F32, name="y%d%d" % (fb, h))
+            for e in range(E):
+                acc[(fb, e)] = psum.tile([P, C], F32, name="acc%d%d" % (fb, e))
+
+        def multiply(a, experts):
+            for fb in range(2):
+                for e in experts:
+                    nc.tensor.matmul_mx(
+                        out=acc[(fb, e)][:],
+                        lhsT=w_cd[:, e * PASSES + a, fb * P : (fb + 1) * P].bitcast(FP8X4),
+                        lhsT_scale=w_sc[:, e * PASSES + a, fb * P : (fb + 1) * P],
+                        rhs=x_cd[a][:, e * C : (e + 1) * C].bitcast(FP8X4),
+                        rhs_scale=x_sc[a][:, e * C : (e + 1) * C],
+                        start=(a == 0),
+                        stop=(a == PASSES - 1),
+                    )
+                    if a == PASSES - 1:
+                        nc.scalar.copy(out=y_sb[(fb, e // 2)][:, (e % 2) * C : (e % 2 + 1) * C], in_=acc[(fb, e)][:])
+
+        def scatter(fb, h):
+            nc.vector.tensor_tensor(
+                out=window[fb][:].indirect(lists[:, h * (HALF // 16) : (h + 1) * (HALF // 16)]),
+                in0=y_sb[(fb, h)][:],
+                in1=gate_sb[fb][:, h * HALF : (h + 1) * HALF],
+                op=MULT,
+            )
+
+        gather(0, 0, 0, 512)
+        gather(0, 1, 0, 512)
+        interleave(0, 0, 512)
+        gather(1, 0, 0, 512)
+        gather(1, 1, 0, 256)
+        interleave(1, 0, 256)
+        quantize(0, 0, 512)
+        multiply(0, (0, 1))
+        quantize(1, 0, 256)
+        multiply(1, (0, 1))
+        multiply(0, (2, 3))
+        gather(1, 1, 256, 512)
+        interleave(1, 256, 512)
+        scatter(0, 0)
+        quantize(1, 256, 512)
+        multiply(1, (2, 3))
+        scatter(1, 0)
+        scatter(0, 1)
+        nc.sync.dma_start(out[0:P, :], window[0][:])
+        scatter(1, 1)
+        nc.sync.dma_start(out[P : 2 * P, :], window[1][:])

@@ -110,9 +110,12 @@ def tile_routed_moe_kernel(tc, xT, w_words, w_scales, gate, offs, out):
             win = words[:, m * T : m * T + width]
             nc.vector.tensor_copy(out=picked[a][:, u, j0:j1], in_=win.indirect(lists[:, j0 // 16 : j1 // 16]))
 
-        def interleave(a, j0, j1):
+        def interleave(a, j0, j1, eng="s"):
             dst = grouped[a][:].rearrange("p c j -> p (c j)").bitcast(U32).rearrange("p (c u) -> p c u", u=2)
-            nc.scalar.copy(out=dst[:, j0:j1, :], in_=picked[a][:, :, j0:j1].rearrange("p u c -> p c u"))
+            if eng == "s":
+                nc.scalar.copy(out=dst[:, j0:j1, :], in_=picked[a][:, :, j0:j1].rearrange("p u c -> p c u"))
+            else:
+                nc.gpsimd.tensor_copy(out=dst[:, j0:j1, :], in_=picked[a][:, :, j0:j1].rearrange("p u c -> p c u"))
 
         def quantize(a, j0, j1):
             nc.vector.quantize_mx(
@@ -156,17 +159,19 @@ def tile_routed_moe_kernel(tc, xT, w_words, w_scales, gate, offs, out):
 
         gather(0, 0, 0, 512)
         gather(0, 1, 0, 512)
-        interleave(0, 0, 512)
+        interleave(0, 0, 256, "s")
+        interleave(0, 256, 512, "g")
         gather(1, 0, 0, 512)
         gather(1, 1, 0, 256)
         interleave(1, 0, 256)
-        quantize(0, 0, 512)
+        quantize(0, 0, 256)
         multiply(0, (0, 1))
         quantize(1, 0, 256)
         multiply(1, (0, 1))
-        multiply(0, (2, 3))
         gather(1, 1, 256, 512)
         interleave(1, 256, 512)
+        quantize(0, 256, 512)
+        multiply(0, (2, 3))
         scatter(0, 0)
         quantize(1, 256, 512)
         multiply(1, (2, 3))

@@ -21,9 +21,9 @@ HALF = 256
 
 CAST = {
     (0, 0): [("v", 0, 320), ("s", 320, 512)],
-    (0, 1): [("s", 0, 288), ("g", 288, 512)],
-    (1, 0): [("s", 0, 288), ("g", 288, 512)],
-    (1, 1): [("s", 0, 288), ("g", 288, 512)],
+    (0, 1): [("s", 0, 224), ("g", 224, 512)],
+    (1, 0): [("s", 0, 224), ("g", 224, 512)],
+    (1, 1): [("s", 0, 224), ("g", 224, 512)],
 }
 LOADS = [
     ("x", 0, 0, 0, 512),

@@ -177,6 +177,6 @@ def tile_routed_moe_kernel(tc, xT, w_words, w_scales, gate, offs, out):
         multiply(1, (2, 3))
         scatter(1, 0)
         scatter(0, 1)
-        nc.sync.dma_start(out[0:P, :], window[0][:])
+        nc.scalar.dma_start(out[0:P, :], window[0][:])
         scatter(1, 1)
-        nc.sync.dma_start(out[P : 2 * P, :], window[1][:])
+        nc.scalar.dma_start(out[P : 2 * P, :], window[1][:])

@@ -21,9 +21,9 @@ HALF = 256
 
 CAST = {
     (0, 0): [("v", 0, 320), ("s", 320, 512)],
-    (0, 1): [("s", 0, 224), ("g", 224, 512)],
-    (1, 0): [("s", 0, 224), ("g", 224, 512)],
-    (1, 1): [("s", 0, 224), ("g", 224, 512)],
+    (0, 1): [("s", 0, 288), ("g", 288, 512)],
+    (1, 0): [("s", 0, 288), ("g", 288, 512)],
+    (1, 1): [("s", 0, 288), ("g", 288, 512)],
 }
 LOADS = [
     ("x", 0, 0, 0, 512),
@@ -98,30 +98,49 @@ def tile_routed_moe_kernel(tc, xT, w_words, w_scales, gate, offs, out):
 
         grouped, x_cd, x_sc = [], [], []
         for a in range(PASSES):
-            grouped.append(held.tile([P, T, 4], BF16, name="grouped%d" % a, align_bytes=64))
-            x_cd.append(held.tile([P, T], U32, name="x_cd%d" % a, align_bytes=64))
-            x_sc.append(held.tile([P, T], U8, name="x_sc%d" % a, align_bytes=64))
+            grouped.append(
+                [
+                    held.tile([P, HALF, 4], BF16, name="grouped%d%d" % (a, h), tag="late" if (a, h) == (0, 0) else "grouped%d%d" % (a, h), align_bytes=64)
+                    for h in range(2 - a)
+                ]
+            )
+            x_cd.append(
+                [
+                    held.tile([P, HALF], U32, name="x_cd%d%d" % (a, h), tag="turn" if (a, h) == (1, 0) else "x_cd%d%d" % (a, h), align_bytes=64)
+                    for h in range(2)
+                ]
+            )
+            x_sc.append([held.tile([P, HALF], U8, name="x_sc%d%d" % (a, h), align_bytes=64) for h in range(2)])
 
-        picked = [held.tile([P, 2, T], U32, name="picked%d" % a) for a in range(PASSES)]
+        picked = [held.tile([P, 2, T], U32, name="picked0")]
 
         def gather(a, u, j0, j1):
             m = slot_of(a, u)
             width = T if j1 - j0 < T else 2 * T
             win = words[:, m * T : m * T + width]
-            nc.vector.tensor_copy(out=picked[a][:, u, j0:j1], in_=win.indirect(lists[:, j0 // 16 : j1 // 16]))
+            b = a * HALF
+            nc.vector.tensor_copy(out=picked[a][:, u, j0 - b : j1 - b], in_=win.indirect(lists[:, j0 // 16 : j1 // 16]))
+
+        def gather_step(a, u, j0, j1):
+            m = slot_of(a, u)
+            dst = grouped[a][j0 // HALF][:].rearrange("p c j -> p (c j)").bitcast(U32).rearrange("p (c u) -> p c u", u=2)
+            nc.vector.tensor_copy(
+                out=dst[:, :, u], in_=words[:, m * T : (m + 1) * T].indirect(lists[:, j0 // 16 : j1 // 16])
+            )
 
         def interleave(a, j0, j1, eng="s"):
-            dst = grouped[a][:].rearrange("p c j -> p (c j)").bitcast(U32).rearrange("p (c u) -> p c u", u=2)
+            b = a * HALF
+            dst = grouped[a][j0 // HALF][:].rearrange("p c j -> p (c j)").bitcast(U32).rearrange("p (c u) -> p c u", u=2)
             if eng == "s":
-                nc.scalar.copy(out=dst[:, j0:j1, :], in_=picked[a][:, :, j0:j1].rearrange("p u c -> p c u"))
+                nc.scalar.copy(out=dst[:], in_=picked[a][:, :, j0 - b : j1 - b].rearrange("p u c -> p c u"))
             else:
-                nc.gpsimd.tensor_copy(out=dst[:, j0:j1, :], in_=picked[a][:, :, j0:j1].rearrange("p u c -> p c u"))
+                nc.gpsimd.tensor_copy(out=dst[:], in_=picked[a][:, :, j0 - b : j1 - b].rearrange("p u c -> p c u"))
 
-        def quantize(a, j0, j1):
+        def quantize(a, h):
             nc.vector.quantize_mx(
-                out=x_cd[a][:, j0:j1].bitcast(FP8X4),
-                scales=x_sc[a][:, j0:j1],
-                in_=grouped[a][:, j0:j1, :].rearrange("p c j -> p (c j)"),
+                out=x_cd[a][h][:].bitcast(FP8X4),
+                scales=x_sc[a][h][:],
+                in_=grouped[a][h][:].rearrange("p c j -> p (c j)"),
             )
 
         acc = {}
@@ -141,8 +160,8 @@ def tile_routed_moe_kernel(tc, xT, w_words, w_scales, gate, offs, out):
                         out=acc[(fb, e)][:],
                         lhsT=w_cd[:, e * PASSES + a, fb * P : (fb + 1) * P].bitcast(FP8X4),
                         lhsT_scale=w_sc[:, e * PASSES + a, fb * P : (fb + 1) * P],
-                        rhs=x_cd[a][:, e * C : (e + 1) * C].bitcast(FP8X4),
-                        rhs_scale=x_sc[a][:, e * C : (e + 1) * C],
+                        rhs=x_cd[a][e // 2][:, (e % 2) * C : (e % 2 + 1) * C].bitcast(FP8X4),
+                        rhs_scale=x_sc[a][e // 2][:, (e % 2) * C : (e % 2 + 1) * C],
                         start=(a == 0),
                         stop=(a == PASSES - 1),
                     )
@@ -161,19 +180,21 @@ def tile_routed_moe_kernel(tc, xT, w_words, w_scales, gate, offs, out):
         gather(0, 1, 0, 512)
         interleave(0, 0, 256, "s")
         interleave(0, 256, 512, "g")
-        gather(1, 0, 0, 512)
-        gather(1, 1, 0, 256)
-        interleave(1, 0, 256)
-        quantize(0, 0, 256)
+        gather_step(1, 0, 0, 256)
+        gather_step(1, 1, 0, 256)
+        quantize(0, 0)
         multiply(0, (0, 1))
-        quantize(1, 0, 256)
+        quantize(1, 0)
         multiply(1, (0, 1))
+        picked.append(held.tile([P, 2, HALF], U32, name="picked1", tag="late", align_bytes=64))
+        gather(1, 0, 256, 512)
         gather(1, 1, 256, 512)
+        grouped[1].append(held.tile([P, HALF, 4], BF16, name="grouped11", tag="turn", align_bytes=64))
         interleave(1, 256, 512)
-        quantize(0, 256, 512)
+        quantize(0, 1)
         multiply(0, (2, 3))
         scatter(0, 0)
-        quantize(1, 256, 512)
+        quantize(1, 1)
         multiply(1, (2, 3))
         scatter(1, 0)
         scatter(0, 1)

@@ -23,7 +23,7 @@ CAST = {
     (0, 0): [("v", 0, 320), ("s", 320, 512)],
     (0, 1): [("s", 0, 288), ("g", 288, 512)],
     (1, 0): [("s", 0, 288), ("g", 288, 512)],
-    (1, 1): [("s", 0, 288), ("g", 288, 512)],
+    (1, 1): [("s", 0, 256), ("g", 256, 512)],
 }
 LOADS = [
     ("x", 0, 0, 0, 512),
@@ -96,14 +96,16 @@ def tile_routed_moe_kernel(tc, xT, w_words, w_scales, gate, offs, out):
                             out=pairs[:, m, t0:t1, :], in0=src[:, t0:t1, :], scalar1=1.0, scalar2=0.0, op0=MULT, op1=ADD
                         )
 
+        shared = held.tile([P, C + T], U32, name="shared", align_bytes=64)
         grouped, x_cd, x_sc = [], [], []
         for a in range(PASSES):
-            grouped.append(
-                [
-                    held.tile([P, HALF, 4], BF16, name="grouped%d%d" % (a, h), tag="late" if (a, h) == (0, 0) else "grouped%d%d" % (a, h), align_bytes=64)
-                    for h in range(2 - a)
-                ]
-            )
+            grouped.append([])
+            for h in range(2 - a):
+                if (a, h) == (0, 0):
+                    grouped[a].append(shared[:, C : C + T].bitcast(BF16).rearrange("p (c j) -> p c j", j=4))
+                else:
+                    own = held.tile([P, HALF, 4], BF16, name="grouped%d%d" % (a, h), align_bytes=64)
+                    grouped[a].append(own[:])
             x_cd.append(
                 [
                     held.tile([P, HALF], U32, name="x_cd%d%d" % (a, h), tag="turn" if (a, h) == (1, 0) else "x_cd%d%d" % (a, h), align_bytes=64)
@@ -112,7 +114,8 @@ def tile_routed_moe_kernel(tc, xT, w_words, w_scales, gate, offs, out):
             )
             x_sc.append([held.tile([P, HALF], U8, name="x_sc%d%d" % (a, h), align_bytes=64) for h in range(2)])
 
-        picked = [held.tile([P, 2, T], U32, name="picked0")]
+        picked0 = held.tile([P, 2, T], U32, name="picked0")
+        picked = [picked0[:], shared[:, 0 : 2 * HALF].rearrange("p (u c) -> p u c", u=2)]
 
         def gather(a, u, j0, j1):
             m = slot_of(a, u)
@@ -123,24 +126,24 @@ def tile_routed_moe_kernel(tc, xT, w_words, w_scales, gate, offs, out):
 
         def gather_step(a, u, j0, j1):
             m = slot_of(a, u)
-            dst = grouped[a][j0 // HALF][:].rearrange("p c j -> p (c j)").bitcast(U32).rearrange("p (c u) -> p c u", u=2)
+            dst = grouped[a][j0 // HALF].rearrange("p c j -> p (c j)").bitcast(U32).rearrange("p (c u) -> p c u", u=2)
             nc.vector.tensor_copy(
                 out=dst[:, :, u], in_=words[:, m * T : (m + 1) * T].indirect(lists[:, j0 // 16 : j1 // 16])
             )
 
         def interleave(a, j0, j1, eng="s"):
             b = a * HALF
-            dst = grouped[a][j0 // HALF][:].rearrange("p c j -> p (c j)").bitcast(U32).rearrange("p (c u) -> p c u", u=2)
+            dst = grouped[a][j0 // HALF].rearrange("p c j -> p (c j)").bitcast(U32).rearrange("p (c u) -> p c u", u=2)
             if eng == "s":
-                nc.scalar.copy(out=dst[:], in_=picked[a][:, :, j0 - b : j1 - b].rearrange("p u c -> p c u"))
+                nc.scalar.copy(out=dst, in_=picked[a][:, :, j0 - b : j1 - b].rearrange("p u c -> p c u"))
             else:
-                nc.gpsimd.tensor_copy(out=dst[:], in_=picked[a][:, :, j0 - b : j1 - b].rearrange("p u c -> p c u"))
+                nc.gpsimd.tensor_copy(out=dst, in_=picked[a][:, :, j0 - b : j1 - b].rearrange("p u c -> p c u"))
 
         def quantize(a, h):
             nc.vector.quantize_mx(
                 out=x_cd[a][h][:].bitcast(FP8X4),
                 scales=x_sc[a][h][:],
-                in_=grouped[a][h][:].rearrange("p c j -> p (c j)"),
+                in_=grouped[a][h].rearrange("p c j -> p (c j)"),
             )
 
         acc = {}
@@ -181,15 +184,16 @@ def tile_routed_moe_kernel(tc, xT, w_words, w_scales, gate, offs, out):
         interleave(0, 0, 256, "s")
         interleave(0, 256, 512, "g")
         gather_step(1, 0, 0, 256)
+        gather(1, 0, 256, 384)
         gather_step(1, 1, 0, 256)
         quantize(0, 0)
         multiply(0, (0, 1))
         quantize(1, 0)
         multiply(1, (0, 1))
-        picked.append(held.tile([P, 2, HALF], U32, name="picked1", tag="late", align_bytes=64))
-        gather(1, 0, 256, 512)
+        gather(1, 0, 384, 512)
         gather(1, 1, 256, 512)
-        grouped[1].append(held.tile([P, HALF, 4], BF16, name="grouped11", tag="turn", align_bytes=64))
+        grouped11 = held.tile([P, HALF, 4], BF16, name="grouped11", tag="turn", align_bytes=64)
+        grouped[1].append(grouped11[:])
         interleave(1, 256, 512)
         quantize(0, 1)
         multiply(0, (2, 3))

@@ -32,9 +32,10 @@ LOADS = [
     ("x", 1, 0, 0, 512),
     ("x", 1, 1, 0, 512),
     ("s", 0, 0, 0, 0),
-    ("w", 0, 2, 0, 0),
+    ("w", 0, 2, 0, 1),
+    ("w", 0, 2, 1, 2),
     ("g", 0, 0, 0, 0),
-    ("w", 2, 4, 0, 0),
+    ("w", 2, 4, 0, 2),
     ("g", 1, 0, 0, 0),
 ]
 
@@ -69,10 +70,15 @@ def tile_routed_moe_kernel(tc, xT, w_words, w_scales, gate, offs, out):
                         w_scales[:, :, 4 * q : 4 * q + 4, :].rearrange("e a r n -> r (e a) n").bitcast(I32),
                     )
             elif what == "w":
-                nc.sync.dma_start(
-                    w_cd[:, i * PASSES : j * PASSES, :],
-                    w_words[i:j].rearrange("e a p n r -> p (e a) (n r)").bitcast(I32),
-                )
+                codes = w_cd[:].rearrange("p (e a) n -> p e a n", a=PASSES)[:, i:j, t0:t1, :]
+                view = w_words[i:j, t0:t1].rearrange("e a p n r -> p e a (n r)").bitcast(I32)
+                if t1 - t0 == 1:
+                    nc.sync.dma_start(codes[:, :, 0, :], view[:, :, 0, :])
+                else:
+                    nc.sync.dma_start(
+                        w_cd[:, i * PASSES : j * PASSES, :],
+                        w_words[i:j].rearrange("e a p n r -> p (e a) (n r)").bitcast(I32),
+                    )
             else:
                 nc.sync.dma_start(gate_sb[i][:], gate[i * P : (i + 1) * P, :])
 

@@ -162,8 +162,8 @@ def tile_routed_moe_kernel(tc, xT, w_words, w_scales, gate, offs, out):
             for e in range(E):
                 acc[(fb, e)] = psum.tile([P, C], F32, name="acc%d%d" % (fb, e))
 
-        def multiply(a, experts):
-            for fb in range(2):
+        def multiply(a, experts, blocks=(0, 1)):
+            for fb in blocks:
                 for e in experts:
                     nc.tensor.matmul_mx(
                         out=acc[(fb, e)][:],
@@ -193,9 +193,11 @@ def tile_routed_moe_kernel(tc, xT, w_words, w_scales, gate, offs, out):
         gather(1, 0, 256, 384)
         gather_step(1, 1, 0, 256)
         quantize(0, 0)
-        multiply(0, (0, 1))
+        multiply(0, (0, 1), (0,))
         quantize(1, 0)
-        multiply(1, (0, 1))
+        multiply(1, (0, 1), (0,))
+        multiply(0, (0, 1), (1,))
+        multiply(1, (0, 1), (1,))
         gather(1, 0, 384, 512)
         gather(1, 1, 256, 512)
         grouped11 = held.tile([P, HALF, 4], BF16, name="grouped11", tag="turn", align_bytes=64)

@@ -114,7 +114,7 @@ def tile_routed_moe_kernel(tc, xT, w_words, w_scales, gate, offs, out):
                     grouped[a].append(own[:])
             x_cd.append(
                 [
-                    held.tile([P, HALF], U32, name="x_cd%d%d" % (a, h), tag="turn" if (a, h) == (1, 0) else "x_cd%d%d" % (a, h), align_bytes=64)
+                    held.tile([P, HALF], U32, name="x_cd%d%d" % (a, h), tag="turn" if (a, h) == (0, 0) else "x_cd%d%d" % (a, h), align_bytes=64)
                     for h in range(2)
                 ]
             )
@@ -160,7 +160,8 @@ def tile_routed_moe_kernel(tc, xT, w_words, w_scales, gate, offs, out):
             for h in range(2):
                 y_sb[(fb, h)] = held.tile([P, HALF], F32, name="y%d%d" % (fb, h))
             for e in range(E):
-                acc[(fb, e)] = psum.tile([P, C], F32, name="acc%d%d" % (fb, e))
+                if fb == 0 or e >= 2:
+                    acc[(fb, e)] = psum.tile([P, C], F32, name="acc%d%d" % (fb, e))
 
         def multiply(a, experts, blocks=(0, 1)):
             for fb in blocks:
@@ -196,6 +197,8 @@ def tile_routed_moe_kernel(tc, xT, w_words, w_scales, gate, offs, out):
         multiply(0, (0, 1), (0,))
         quantize(1, 0)
         multiply(1, (0, 1), (0,))
+        for e in range(2):
+            acc[(1, e)] = psum.tile([P, C], F32, name="acc1%d" % e, tag="acc0%d" % e)
         multiply(0, (0, 1), (1,))
         multiply(1, (0, 1), (1,))
         gather(1, 0, 384, 512)

from contextlib import ExitStack

import concourse.mybir as mybir

K, T, E, C, N = 1024, 512, 4, 128, 256
FLOPS = 2 * K * N * E * C

F32 = mybir.dt.float32
BF16 = mybir.dt.bfloat16
U32 = mybir.dt.uint32
I32 = mybir.dt.int32
U16 = mybir.dt.uint16
U8 = mybir.dt.uint8
FP8X4 = mybir.dt.float8_e4m3fn_x4
MULT = mybir.AluOpType.mult
ADD = mybir.AluOpType.add

P = 128
PASSES = K // 512
HALF = 256

CAST = {
    (0, 0): [("v", 0, 320), ("s", 320, 512)],
    (0, 1): [("s", 0, 288), ("g", 288, 512)],
    (1, 0): [("s", 0, 288), ("g", 288, 512)],
    (1, 1): [("s", 0, 256), ("g", 256, 512)],
}
LOADS = [
    ("x", 0, 0, 0, 512),
    ("o", 0, 0, 0, 0),
    ("x", 0, 1, 0, 512),
    ("x", 1, 0, 0, 512),
    ("x", 1, 1, 0, 512),
    ("s", 0, 0, 0, 0),
    ("w", 0, 2, 0, 1),
    ("w", 0, 2, 1, 2),
    ("g", 0, 0, 0, 0),
    ("w", 2, 4, 0, 2),
    ("g", 1, 0, 0, 0),
]


def tile_routed_moe_kernel(tc, xT, w_words, w_scales, gate, offs, out):
    nc = tc.nc
    with ExitStack() as ctx:
        held = ctx.enter_context(tc.tile_pool(name="held", bufs=1))
        psum = ctx.enter_context(tc.psum_pool(name="psum", bufs=1))

        lists = held.tile([P, T // 16], U16, name="lists")

        x_view = xT.rearrange("(a p u e) t -> a u p e t", a=PASSES, p=P, u=2, e=2)
        raw = {}
        for a in range(PASSES):
            for u in range(2):
                raw[(a, u)] = held.tile([P, 2, T], F32, name="raw%d%d" % (a, u))
        w_sc = held.tile([P, E * PASSES, N], U8, name="w_sc", align_bytes=64)
        nc.vector.memset(w_sc[:].rearrange("p g n -> p (g n)").bitcast(I32), 0)
        w_cd = held.tile([P, E * PASSES, N], I32, name="w_cd", align_bytes=64)
        gate_sb = [held.tile([P, T], F32, name="gate%d" % fb) for fb in range(2)]

        for what, i, j, t0, t1 in LOADS:
            if what == "o":
                nc.sync.dma_start(lists[:], offs)
            elif what == "x":
                nc.sync.dma_start(raw[(i, j)][:, :, t0:t1], x_view[i, j][:, :, t0:t1])
            elif what == "s":
                for q in range(4):
                    nc.sync.dma_start(
                        w_sc[32 * q : 32 * q + 4].bitcast(I32),
                        w_scales[:, :, 4 * q : 4 * q + 4, :].rearrange("e a r n -> r (e a) n").bitcast(I32),
                    )
            elif what == "w":
                codes = w_cd[:].rearrange("p (e a) n -> p e a n", a=PASSES)[:, i:j, t0:t1, :]
                view = w_words[i:j, t0:t1].rearrange("e a p n r -> p e a (n r)").bitcast(I32)
                if t1 - t0 == 1:
                    nc.sync.dma_start(codes[:, :, 0, :], view[:, :, 0, :])
                else:
                    nc.sync.dma_start(
                        w_cd[:, i * PASSES : j * PASSES, :],
                        w_words[i:j].rearrange("e a p n r -> p (e a) (n r)").bitcast(I32),
                    )
            else:
                nc.sync.dma_start(gate_sb[i][:], gate[i * P : (i + 1) * P, :])

        pairs = held.tile([P, 5, T, 2], BF16, name="pairs")
        words = pairs[:].rearrange("p m t e -> p (m t e)").bitcast(U32)

        def slot_of(a, u):
            return 3 - (2 * a + u)

        for a in range(PASSES):
            for u in range(2):
                src = raw[(a, u)][:].rearrange("p e t -> p t e")
                m = slot_of(a, u)
                for eng, t0, t1 in CAST[(a, u)]:
                    if eng == "v":
                        nc.vector.tensor_copy(out=pairs[:, m, t0:t1, :], in_=src[:, t0:t1, :])
                    elif eng == "s":
                        nc.scalar.copy(out=pairs[:, m, t0:t1, :], in_=src[:, t0:t1, :])
                    else:
                        nc.gpsimd.tensor_scalar(
                            out=pairs[:, m, t0:t1, :], in0=src[:, t0:t1, :], scalar1=1.0, scalar2=0.0, op0=MULT, op1=ADD
                        )

        shared = held.tile([P, C + T], U32, name="shared", align_bytes=64)
        grouped, x_cd, x_sc = [], [], []
        for a in range(PASSES):
            grouped.append([])
            for h in range(2 - a):
                if (a, h) == (0, 0):
                    grouped[a].append(shared[:, C : C + T].bitcast(BF16).rearrange("p (c j) -> p c j", j=4))
                else:
                    own = held.tile([P, HALF, 4], BF16, name="grouped%d%d" % (a, h), align_bytes=64)
                    grouped[a].append(own[:])
            x_cd.append(
                [
                    held.tile([P, HALF], U32, name="x_cd%d%d" % (a, h), tag="turn" if (a, h) == (0, 0) else "x_cd%d%d" % (a, h), align_bytes=64)
                    for h in range(2)
                ]
            )
            x_sc.append([held.tile([P, HALF], U8, name="x_sc%d%d" % (a, h), align_bytes=64) for h in range(2)])

        picked0 = held.tile([P, 2, T], U32, name="picked0")
        picked = [picked0[:], shared[:, 0 : 2 * HALF].rearrange("p (u c) -> p u c", u=2)]

        def gather(a, u, j0, j1):
            m = slot_of(a, u)
            width = T if j1 - j0 < T else 2 * T
            win = words[:, m * T : m * T + width]
            b = a * HALF
            nc.vector.tensor_copy(out=picked[a][:, u, j0 - b : j1 - b], in_=win.indirect(lists[:, j0 // 16 : j1 // 16]))

        def gather_step(a, u, j0, j1):
            m = slot_of(a, u)
            dst = grouped[a][j0 // HALF].rearrange("p c j -> p (c j)").bitcast(U32).rearrange("p (c u) -> p c u", u=2)
            nc.vector.tensor_copy(
                out=dst[:, :, u], in_=words[:, m * T : (m + 1) * T].indirect(lists[:, j0 // 16 : j1 // 16])
            )

        def interleave(a, j0, j1, eng="s"):
            b = a * HALF
            dst = grouped[a][j0 // HALF].rearrange("p c j -> p (c j)").bitcast(U32).rearrange("p (c u) -> p c u", u=2)
            if eng == "s":
                nc.scalar.copy(out=dst, in_=picked[a][:, :, j0 - b : j1 - b].rearrange("p u c -> p c u"))
            else:
                nc.gpsimd.tensor_copy(out=dst, in_=picked[a][:, :, j0 - b : j1 - b].rearrange("p u c -> p c u"))

        def quantize(a, h):
            nc.vector.quantize_mx(
                out=x_cd[a][h][:].bitcast(FP8X4),
                scales=x_sc[a][h][:],
                in_=grouped[a][h].rearrange("p c j -> p (c j)"),
            )

        acc = {}
        y_sb = {}
        window = []
        for fb in range(2):
            window.append(held.tile([P, T], F32, name="window%d" % fb))
            for h in range(2):
                y_sb[(fb, h)] = held.tile([P, HALF], F32, name="y%d%d" % (fb, h))
            for e in range(E):
                if fb == 0 or e >= 2:
                    acc[(fb, e)] = psum.tile([P, C], F32, name="acc%d%d" % (fb, e))

        def multiply(a, experts, blocks=(0, 1)):
            for fb in blocks:
                for e in experts:
                    nc.tensor.matmul_mx(
                        out=acc[(fb, e)][:],
                        lhsT=w_cd[:, e * PASSES + a, fb * P : (fb + 1) * P].bitcast(FP8X4),
                        lhsT_scale=w_sc[:, e * PASSES + a, fb * P : (fb + 1) * P],
                        rhs=x_cd[a][e // 2][:, (e % 2) * C : (e % 2 + 1) * C].bitcast(FP8X4),
                        rhs_scale=x_sc[a][e // 2][:, (e % 2) * C : (e % 2 + 1) * C],
                        start=(a == 0),
                        stop=(a == PASSES - 1),
                    )
                    if a == PASSES - 1:
                        nc.scalar.copy(out=y_sb[(fb, e // 2)][:, (e % 2) * C : (e % 2 + 1) * C], in_=acc[(fb, e)][:])

        def scatter(fb, h):
            nc.vector.tensor_tensor(
                out=window[fb][:].indirect(lists[:, h * (HALF // 16) : (h + 1) * (HALF // 16)]),
                in0=y_sb[(fb, h)][:],
                in1=gate_sb[fb][:, h * HALF : (h + 1) * HALF],
                op=MULT,
            )

        gather(0, 0, 0, 512)
        gather(0, 1, 0, 512)
        interleave(0, 0, 256, "s")
        interleave(0, 256, 512, "g")
        gather_step(1, 0, 0, 256)
        gather(1, 0, 256, 384)
        gather_step(1, 1, 0, 256)
        quantize(0, 0)
        multiply(0, (0, 1), (0,))
        quantize(1, 0)
        multiply(1, (0, 1), (0,))
        for e in range(2):
            acc[(1, e)] = psum.tile([P, C], F32, name="acc1%d" % e, tag="acc0%d" % e)
        multiply(0, (0, 1), (1,))
        multiply(1, (0, 1), (1,))
        gather(1, 0, 384, 512)
        gather(1, 1, 256, 512)
        grouped11 = held.tile([P, HALF, 4], BF16, name="grouped11", tag="turn", align_bytes=64)
        grouped[1].append(grouped11[:])
        interleave(1, 256, 512)
        quantize(0, 1)
        multiply(0, (2, 3))
        scatter(0, 0)
        quantize(1, 1)
        multiply(1, (2, 3))
        scatter(1, 0)
        scatter(0, 1)
        nc.scalar.dma_start(out[0:P, :], window[0][:])
        scatter(1, 1)
        nc.scalar.dma_start(out[P : 2 * P, :], window[1][:])
